import numpy as np
import ml_dtypes


def mxq(x, axis, fmt="e4m3"):
    dtype, down = {"e4m3": (ml_dtypes.float8_e4m3fn, 7), "e5m2": (ml_dtypes.float8_e5m2, 14)}[fmt]
    v = np.moveaxis(np.asarray(x, np.float32).astype(ml_dtypes.bfloat16).astype(np.float64), axis, -1)
    blocks = v.reshape(v.shape[:-1] + (-1, 32))
    amax = np.abs(blocks).max(-1, keepdims=True)
    byte = np.maximum(np.where(amax > 0, np.frexp(amax)[1] - 1 + 127, 0) - down, 1)
    scale = np.exp2(byte - 127.0)
    codes = (blocks / scale).astype(np.float32).astype(dtype).astype(np.float64)
    return np.moveaxis((codes * scale).reshape(v.shape), -1, axis)


WIDE = False


def mx_kscale(k):
    if not WIDE:
        return np.ones(k)
    levels = np.array([30, -30])
    if k % 512:
        return np.exp2(np.random.permutation(np.resize(levels, k // 32))).repeat(32)
    a = np.empty((k // 512, 16))
    for p in range(k // 512):
        a[p, :8] = np.random.permutation(np.resize(levels, 8))
        for g in range(8):
            far = levels[np.abs(levels - a[p, g]) >= 10]
            a[p, g + 8] = far[np.random.randint(len(far))]
    return np.exp2(a.ravel()).repeat(32)


def f64(x):
    return np.asarray(x).astype(np.float64)


def striped(idx):
    return np.tile(np.asarray(idx).reshape(-1, 16).T, (8, 1)).astype(np.uint16)


def unstriped(offs):
    return offs[:16].T.reshape(-1).astype(np.int64)


K, J, N, T, V, C, E = 256, 1024, 256, 2048, 2048, 128, 128


def setup_inputs():
    n = np.random.standard_normal
    idx = np.random.permutation(T)[:J]
    idx2 = np.random.permutation(T)[:J]
    idx3 = np.random.permutation(V)[:J]
    idx4 = np.random.permutation(N)[:E]
    fj = mx_kscale(J)
    return {
        "xf": (n((K, T))).astype(np.float32),
        "ra": (np.random.uniform(0.5, 1.5, (1, J)) * fj).astype(np.float32),
        "gt": (n((N, V)) * np.exp(0.5 * n((1, V)))).astype(np.float32),
        "rb": (np.random.uniform(0.5, 1.5, (1, J)) / fj).astype(np.float32),
        "old": (0.5 * n((K, E))).astype(np.float32),
        "offs": striped(idx),
        "offs2": striped(idx2),
        "offs3": striped(idx3),
        "offs4": striped(idx4),
    }


def reference(xf, ra, gt, rb, old, offs, offs2, offs3, offs4):
    idx = unstriped(offs)
    idx2 = unstriped(offs2)
    idx3 = unstriped(offs3)
    idx4 = unstriped(offs4)
    us = (f64(xf)[:, idx] - f64(xf)[:, idx2]) * f64(ra)
    uj = us.T
    gg = f64(gt)[:, idx3]
    c1 = gg.reshape(N, C, J // C).mean(axis=2)
    c2 = np.repeat(c1, J // C, axis=1)
    gs = (gg - c2) * f64(rb)
    gj = gs.T
    ujq = mxq(uj, 0, "e4m3")
    gjq = mxq(gj, 0, "e5m2")
    w = ujq.T @ gjq
    y = 0.04 * w[:, idx4] + f64(old)
    return y

@@ -1,0 +1,165 @@
+from contextlib import ExitStack
+
+import concourse.mybir as mybir
+from concourse.masks import make_identity
+
+K, J, N, T, E = 256, 1024, 256, 2048, 128
+SET = 8
+FLOPS = 2 * K * J * N
+
+F32 = mybir.dt.float32
+BF16 = mybir.dt.bfloat16
+U32 = mybir.dt.uint32
+U16 = mybir.dt.uint16
+U8 = mybir.dt.uint8
+E4M3X4 = mybir.dt.float8_e4m3fn_x4
+E5M2X4 = mybir.dt.float8_e5m2_x4
+ALU = mybir.AluOpType
+COPY = mybir.ActivationFunctionType.Copy
+
+P = 128
+PACK = 4
+PASS = P * PACK
+PASSES = J // PASS
+LANES = 16
+
+
+def tile_list_moment_gaps_centred_columns_kernel(tc, xf, ra, gt, rb, old, offs, offs2, offs3, offs4, out):
+    nc = tc.nc
+    with ExitStack() as ctx:
+        keep = ctx.enter_context(tc.tile_pool(name="keep", bufs=1))
+        psum = ctx.enter_context(tc.psum_pool(name="psum", bufs=1))
+
+        list1 = keep.tile([P, J // LANES], U16, name="list1")
+        list2 = keep.tile([P, J // LANES], U16, name="list2")
+        list3 = keep.tile([P, J // LANES], U16, name="list3")
+        list4 = keep.tile([P, E // LANES], U16, name="list4")
+        x_rows = [keep.tile([P, T], F32, name="x_rows%d" % b) for b in range(2)]
+        g_rows = [keep.tile([P, T], F32, name="g_rows%d" % b) for b in range(2)]
+        ra_slots = keep.tile([P, PASSES, PACK], F32, name="ra_slots")
+        rb_slots = keep.tile([P, PASSES, PACK], F32, name="rb_slots")
+        old_rows = keep.tile([P, 2, E], F32, name="old_rows")
+
+        nc.sync.dma_start(list2[:], offs2)
+        nc.sync.dma_start(x_rows[0][:], xf[0:P, :])
+        nc.sync.dma_start(list1[:], offs)
+        nc.sync.dma_start(x_rows[1][:], xf[P : 2 * P, :])
+        nc.sync.dma_start(ra_slots[:], ra.rearrange("o (a p t) -> p (o a) t", p=P, t=PACK))
+        nc.sync.dma_start(list3[:], offs3)
+        nc.sync.dma_start(g_rows[0][:], gt[0:P, :])
+        nc.sync.dma_start(rb_slots[:], rb.rearrange("o (a p t) -> p (o a) t", p=P, t=PACK))
+        nc.sync.dma_start(g_rows[1][:], gt[P : 2 * P, :])
+        nc.sync.dma_start(list4[:], offs4)
+        nc.sync.dma_start(old_rows[:], old.rearrange("(b p) e -> p b e", p=P))
+
+        ident = keep.tile([P, P], F32, name="ident")
+        make_identity(nc, ident[:])
+
+        def picked(table, offsets, lo, hi):
+            return table[:].indirect(offsets[:, lo // LANES : hi // LANES])
+
+        codes, scales, rounded = {}, {}, {}
+        for side in "ug":
+            for b in range(2):
+                codes[side, b] = keep.tile([P, PASSES * P], U32, name="codes_%s%d" % (side, b), align_bytes=64)
+                scales[side, b] = keep.tile([P, PASSES * P], U8, name="scales_%s%d" % (side, b), align_bytes=64)
+                rounded[side, b] = keep.tile([P, PASSES, P, PACK], BF16, name="rounded_%s%d" % (side, b), align_bytes=64)
+
+        def weigh(side, b, a, bank, weights):
+            nc.vector.tensor_tensor(
+                rounded[side, b][:, a],
+                bank[:].rearrange("p t c -> p c t"),
+                weights[:, a : a + 1, :].to_broadcast([P, P, PACK]),
+                ALU.mult,
+            )
+
+        def quantise(side, b, first, last):
+            cols = slice(first * P, last * P)
+            nc.vector.quantize_mx(
+                out=codes[side, b][:, cols].bitcast(E4M3X4 if side == "u" else E5M2X4),
+                scales=scales[side, b][:, cols],
+                in_=rounded[side, b][:, first:last].rearrange("p a c t -> p (a c t)"),
+            )
+
+        u_banks = {}
+        for b in range(2):
+            second = keep.tile([P, J], F32, name="second%d" % b)
+            gap = keep.tile([P, J], F32, name="gap%d" % b)
+            cuts = [0, 128, PASS, J] if b == 0 else [0, PASS, J]
+            for lo, hi in zip(cuts, cuts[1:]):
+                nc.scalar.activation(second[:, lo:hi], picked(x_rows[b], list2, lo, hi), COPY)
+                nc.vector.tensor_tensor(gap[:, lo:hi], picked(x_rows[b], list1, lo, hi), second[:, lo:hi], ALU.subtract)
+                if hi % PASS == 0:
+                    a = hi // PASS - 1
+                    bank = psum.tile([P, PACK, P], F32, name="u_bank%d%d" % (b, a), tag="bank%d" % (2 * b + a))
+                    for t in range(PACK):
+                        nc.tensor.transpose(bank[:, t, :], gap[:, a * PASS + t : (a + 1) * PASS : PACK], ident[:])
+                    u_banks[b, a] = bank
+
+        g_banks = {}
+
+        def centre(b, a):
+            gg = keep.tile([P, PASS], F32, name="gg%d%d" % (b, a))
+            nc.scalar.activation(gg[:], picked(g_rows[b], list3, a * PASS, (a + 1) * PASS), COPY)
+            sums = keep.tile([P, PASS // SET], F32, name="sums%d%d" % (b, a))
+            nc.vector.tensor_reduce(sums[:], gg[:].rearrange("p (c s) -> p c s", s=SET), mybir.AxisListType.X, ALU.add)
+            less_mean = keep.tile([P, PASS // SET, 2], F32, name="less_mean%d%d" % (b, a))
+            nc.gpsimd.tensor_scalar(
+                less_mean[:], sums[:].unsqueeze(2).to_broadcast([P, PASS // SET, 2]), -1.0 / SET, 0.0, ALU.mult, ALU.add
+            )
+            bank = psum.tile([P, PACK, P], F32, name="g_bank%d%d" % (b, a), tag="bank%d" % (4 + 2 * b + a))
+            for t in range(PACK):
+                nc.tensor.matmul(bank[:, t, :], gg[:, t:PASS:PACK], ident[:], start=(t == 0), stop=False, is_transpose=True)
+            for t in range(PACK):
+                nc.tensor.matmul(
+                    bank[:, t, :],
+                    less_mean[:].rearrange("p c h -> p (c h)"),
+                    ident[:],
+                    start=False,
+                    stop=(t == PACK - 1),
+                    is_transpose=True,
+                )
+            g_banks[b, a] = bank
+
+        for b in range(2):
+            for a in range(PASSES):
+                weigh("u", b, a, u_banks[b, a], ra_slots)
+                centre(b, a)
+        for b in range(2):
+            quantise("u", b, 0, PASSES)
+        for a in range(PASSES):
+            weigh("g", 0, a, g_banks[0, a], rb_slots)
+        weigh("g", 1, 0, g_banks[1, 0], rb_slots)
+        quantise("g", 0, 0, PASSES)
+        quantise("g", 1, 0, 1)
+        weigh("g", 1, 1, g_banks[1, 1], rb_slots)
+        quantise("g", 1, 1, 2)
+
+        w_rows = [keep.tile([P, N], F32, name="w_rows%d" % b) for b in range(2)]
+        w_banks = {}
+        for nb in range(2):
+            for kb in range(2):
+                w_banks[kb, nb] = psum.tile([P, P], F32, name="w_bank%d%d" % (kb, nb), tag="bank%d" % (2 * kb + nb))
+            for a in range(PASSES):
+                cols = slice(a * P, (a + 1) * P)
+                for kb in range(2):
+                    nc.tensor.matmul_mx(
+                        out=w_banks[kb, nb][:],
+                        lhsT=codes["u", kb][:, cols].bitcast(E4M3X4),
+                        lhsT_scale=scales["u", kb][:, cols],
+                        rhs=codes["g", nb][:, cols].bitcast(E5M2X4),
+                        rhs_scale=scales["g", nb][:, cols],
+                        start=(a == 0),
+                        stop=(a == PASSES - 1),
+                    )
+        nc.scalar.copy(w_rows[0][:, 0:P], w_banks[0, 0][:])
+        nc.scalar.copy(w_rows[1][:, 0:P], w_banks[1, 0][:])
+        nc.scalar.copy(w_rows[0][:, P:N], w_banks[0, 1][:])
+        nc.vector.tensor_copy(w_rows[1][:, P:N], w_banks[1, 1][:])
+
+        w_picked = keep.tile([P, 2, E], F32, name="w_picked")
+        nc.scalar.activation(w_picked[:, 0, :], w_rows[0][:].indirect(list4[:]), COPY)
+        nc.vector.tensor_copy(w_picked[:, 1, :], w_rows[1][:].indirect(list4[:]))
+        result = keep.tile([P, 2, E], F32, name="result")
+        nc.vector.scalar_tensor_tensor(result[:], w_picked[:], 0.04, old_rows[:], ALU.mult, ALU.add)
+        nc.sync.dma_start(out.rearrange("(b p) e -> p b e", p=P), result[:])

@@ -22,6 +22,7 @@ PACK = 4
 PASS = P * PACK
 PASSES = J // PASS
 LANES = 16
+SETS = PASS // SET
 
 
 def tile_list_moment_gaps_centred_columns_kernel(tc, xf, ra, gt, rb, old, offs, offs2, offs3, offs4, out):
@@ -29,13 +30,14 @@ def tile_list_moment_gaps_centred_columns_kernel(tc, xf, ra, gt, rb, old, offs, 
     with ExitStack() as ctx:
         keep = ctx.enter_context(tc.tile_pool(name="keep", bufs=1))
         psum = ctx.enter_context(tc.psum_pool(name="psum", bufs=1))
+        late = ctx.enter_context(tc.tile_pool(name="late", bufs=1))
 
         list1 = keep.tile([P, J // LANES], U16, name="list1")
         list2 = keep.tile([P, J // LANES], U16, name="list2")
         list3 = keep.tile([P, J // LANES], U16, name="list3")
         list4 = keep.tile([P, E // LANES], U16, name="list4")
         x_rows = [keep.tile([P, T], F32, name="x_rows%d" % b) for b in range(2)]
-        g_rows = [keep.tile([P, T], F32, name="g_rows%d" % b) for b in range(2)]
+        g_rows = [keep.tile([P, T], F32, name="g_rows0"), late.tile([P, T], F32, name="g_rows1", offset=0, align_bytes=64)]
         ra_slots = keep.tile([P, PASSES, PACK], F32, name="ra_slots")
         rb_slots = keep.tile([P, PASSES, PACK], F32, name="rb_slots")
         old_rows = keep.tile([P, 2, E], F32, name="old_rows")
@@ -47,41 +49,43 @@ def tile_list_moment_gaps_centred_columns_kernel(tc, xf, ra, gt, rb, old, offs, 
         nc.sync.dma_start(ra_slots[:], ra.rearrange("o (a p t) -> p (o a) t", p=P, t=PACK))
         nc.sync.dma_start(list3[:], offs3)
         nc.sync.dma_start(g_rows[0][:], gt[0:P, :])
-        nc.sync.dma_start(rb_slots[:], rb.rearrange("o (a p t) -> p (o a) t", p=P, t=PACK))
         nc.sync.dma_start(g_rows[1][:], gt[P : 2 * P, :])
+        nc.sync.dma_start(rb_slots[:], rb.rearrange("o (a p t) -> p (o a) t", p=P, t=PACK))
         nc.sync.dma_start(list4[:], offs4)
         nc.sync.dma_start(old_rows[:], old.rearrange("(b p) e -> p b e", p=P))
 
         ident = keep.tile([P, P], F32, name="ident")
         make_identity(nc, ident[:])
 
+        table_warm = keep.tile([P, 2], F32, name="table_warm")
+        nc.vector.memset(table_warm[:, 0:1], 0.0)
+        nc.scalar.activation(table_warm[:, 1:2], table_warm[:, 0:1], COPY)
+
         def picked(table, offsets, lo, hi):
             return table[:].indirect(offsets[:, lo // LANES : hi // LANES])
 
-        codes, scales, rounded = {}, {}, {}
+        ra_spread = []
+        for a in range(PASSES):
+            bank = psum.tile([P, PACK, P], F32, name="ra_spread%d" % a, tag="bank%d" % a)
+            for t in range(PACK):
+                nc.tensor.transpose(bank[:, t, :], ra_slots[:, a, t : t + 1].to_broadcast([P, P]), ident[:])
+            ra_spread.append(bank)
+
+        codes, scales, grouped = {}, {}, {}
         for side in "ug":
             for b in range(2):
                 codes[side, b] = keep.tile([P, PASSES * P], U32, name="codes_%s%d" % (side, b), align_bytes=64)
                 scales[side, b] = keep.tile([P, PASSES * P], U8, name="scales_%s%d" % (side, b), align_bytes=64)
-                rounded[side, b] = keep.tile([P, PASSES, P, PACK], BF16, name="rounded_%s%d" % (side, b), align_bytes=64)
-
-        def weigh(side, b, a, bank, weights):
-            nc.vector.tensor_tensor(
-                rounded[side, b][:, a],
-                bank[:].rearrange("p t c -> p c t"),
-                weights[:, a : a + 1, :].to_broadcast([P, P, PACK]),
-                ALU.mult,
-            )
 
         def quantise(side, b, first, last):
             cols = slice(first * P, last * P)
             nc.vector.quantize_mx(
                 out=codes[side, b][:, cols].bitcast(E4M3X4 if side == "u" else E5M2X4),
                 scales=scales[side, b][:, cols],
-                in_=rounded[side, b][:, first:last].rearrange("p a c t -> p (a c t)"),
+                in_=grouped[side, b, first],
             )
 
-        u_banks = {}
+        gaps, pairs = {}, {}
         for b in range(2):
             second = keep.tile([P, J], F32, name="second%d" % b)
             gap = keep.tile([P, J], F32, name="gap%d" % b)
@@ -89,57 +93,118 @@ def tile_list_moment_gaps_centred_columns_kernel(tc, xf, ra, gt, rb, old, offs, 
             for lo, hi in zip(cuts, cuts[1:]):
                 nc.scalar.activation(second[:, lo:hi], picked(x_rows[b], list2, lo, hi), COPY)
                 nc.vector.tensor_tensor(gap[:, lo:hi], picked(x_rows[b], list1, lo, hi), second[:, lo:hi], ALU.subtract)
-                if hi % PASS == 0:
-                    a = hi // PASS - 1
-                    bank = psum.tile([P, PACK, P], F32, name="u_bank%d%d" % (b, a), tag="bank%d" % (2 * b + a))
-                    for t in range(PACK):
-                        nc.tensor.transpose(bank[:, t, :], gap[:, a * PASS + t : (a + 1) * PASS : PACK], ident[:])
-                    u_banks[b, a] = bank
+            gaps[b] = gap
 
-        g_banks = {}
+        def weigh_u(b, a):
+            rounded = keep.tile([P, PASS], BF16, name="rounded_u%d%d" % (b, a), align_bytes=64)
+            nc.vector.tensor_tensor(
+                rounded[:].rearrange("r (u p e) -> r u p e", u=2, e=2),
+                gaps[b][:, a * PASS : (a + 1) * PASS].rearrange("r (p u e) -> r u p e", u=2, e=2),
+                ra_spread[a][:].rearrange("r (u e) p -> r u p e", u=2),
+                ALU.mult,
+            )
+            pairs[b, a] = rounded[:].bitcast(F32)
 
-        def centre(b, a):
-            gg = keep.tile([P, PASS], F32, name="gg%d%d" % (b, a))
-            nc.scalar.activation(gg[:], picked(g_rows[b], list3, a * PASS, (a + 1) * PASS), COPY)
-            sums = keep.tile([P, PASS // SET], F32, name="sums%d%d" % (b, a))
-            nc.vector.tensor_reduce(sums[:], gg[:].rearrange("p (c s) -> p c s", s=SET), mybir.AxisListType.X, ALU.add)
-            less_mean = keep.tile([P, PASS // SET, 2], F32, name="less_mean%d%d" % (b, a))
+        def turn_u(b):
+            bank = psum.tile([P, PASSES, 2, P], F32, name="turned_u%d" % b, tag="bank%d" % (2 + b))
+            for a in range(PASSES):
+                for u in range(2):
+                    nc.tensor.transpose(bank[:, a, u, :], pairs[b, a][:, u * P : (u + 1) * P], ident[:])
+            words = late.tile([P, PASS], F32, name="grouped_u%d" % b, align_bytes=64, offset=b * PASS * 4)
+            nc.scalar.copy(
+                words[:].rearrange("p (a c u) -> p a c u", a=PASSES, u=2), bank[:].rearrange("p a u c -> p a c u")
+            )
+            grouped["u", b, 0] = words[:].bitcast(BF16)
+
+        gg, sums, g_banks = {}, {}, {}
+        LAST = 4 * T
+
+        def pick_g(b, a):
+            if (b, a) == (1, 1):
+                gg[b, a] = late.tile([P, PASS], F32, name="gg%d%d" % (b, a), align_bytes=64, offset=LAST)
+            else:
+                gg[b, a] = keep.tile([P, PASS], F32, name="gg%d%d" % (b, a))
+            nc.scalar.activation(gg[b, a][:], picked(g_rows[b], list3, a * PASS, (a + 1) * PASS), COPY)
+            sums[b, a] = keep.tile([P, SETS], F32, name="sums%d%d" % (b, a))
+            nc.vector.tensor_reduce(
+                sums[b, a][:], gg[b, a][:].rearrange("r (c s) -> r c s", s=SET), mybir.AxisListType.X, ALU.add
+            )
+            dealt = keep.tile([P, PASS], F32, name="dealt%d%d" % (b, a))
             nc.gpsimd.tensor_scalar(
-                less_mean[:], sums[:].unsqueeze(2).to_broadcast([P, PASS // SET, 2]), -1.0 / SET, 0.0, ALU.mult, ALU.add
+                dealt[:].rearrange("r (t q i) -> r q t i", t=PACK, i=4),
+                gg[b, a][:].rearrange("r (q i t) -> r q t i", t=PACK, i=4),
+                1.0,
+                0.0,
+                ALU.mult,
+                ALU.add,
             )
             bank = psum.tile([P, PACK, P], F32, name="g_bank%d%d" % (b, a), tag="bank%d" % (4 + 2 * b + a))
             for t in range(PACK):
-                nc.tensor.matmul(bank[:, t, :], gg[:, t:PASS:PACK], ident[:], start=(t == 0), stop=False, is_transpose=True)
+                nc.tensor.matmul(
+                    bank[:, t, :], dealt[:, t * P : (t + 1) * P], ident[:], start=(t == 0), stop=False, is_transpose=True
+                )
+            g_banks[b, a] = bank
+
+        def centre_g(b, a):
+            place = 2 * PASS * 4 + (2 * b + a) * P * 4
+            less_mean = late.tile([P, SETS, 2], F32, name="less_mean%d%d" % (b, a), align_bytes=64, offset=place)
+            nc.scalar.activation(
+                less_mean[:], sums[b, a][:].unsqueeze(2).to_broadcast([P, SETS, 2]), COPY, scale=-1.0 / SET
+            )
             for t in range(PACK):
                 nc.tensor.matmul(
-                    bank[:, t, :],
-                    less_mean[:].rearrange("p c h -> p (c h)"),
+                    g_banks[b, a][:, t, :],
+                    less_mean[:].rearrange("r c h -> r (c h)"),
                     ident[:],
                     start=False,
                     stop=(t == PACK - 1),
                     is_transpose=True,
                 )
-            g_banks[b, a] = bank
 
-        for b in range(2):
-            for a in range(PASSES):
-                weigh("u", b, a, u_banks[b, a], ra_slots)
-                centre(b, a)
-        for b in range(2):
-            quantise("u", b, 0, PASSES)
-        for a in range(PASSES):
-            weigh("g", 0, a, g_banks[0, a], rb_slots)
-        weigh("g", 1, 0, g_banks[1, 0], rb_slots)
-        quantise("g", 0, 0, PASSES)
+        def weigh_g(b, a):
+            name = "grouped_g%d%d" % (b, a)
+            if b == 0:
+                rounded = late.tile([P, PASS], BF16, name=name, align_bytes=64, offset=LAST + a * PASS * 2)
+            else:
+                rounded = keep.tile([P, PASS], BF16, name=name, align_bytes=64)
+            nc.vector.tensor_tensor(
+                rounded[:].rearrange("p (c t) -> p c t", t=PACK),
+                g_banks[b, a][:].rearrange("p t c -> p c t"),
+                rb_slots[:, a : a + 1, :].to_broadcast([P, P, PACK]),
+                ALU.mult,
+            )
+            grouped["g", b, a] = rounded[:]
+
+        weigh_u(0, 0)
+        weigh_u(0, 1)
+        weigh_u(1, 0)
+        weigh_u(1, 1)
+        pick_g(0, 0)
+        pick_g(0, 1)
+        pick_g(1, 0)
+        pick_g(1, 1)
+        centre_g(0, 0)
+        centre_g(0, 1)
+        turn_u(0)
+        centre_g(1, 0)
+        centre_g(1, 1)
+        turn_u(1)
+        weigh_g(0, 0)
+        weigh_g(0, 1)
+        quantise("u", 0, 0, 2)
+        weigh_g(1, 0)
+        quantise("u", 1, 0, 2)
+        quantise("g", 0, 0, 1)
+        quantise("g", 0, 1, 2)
+        weigh_g(1, 1)
         quantise("g", 1, 0, 1)
-        weigh("g", 1, 1, g_banks[1, 1], rb_slots)
         quantise("g", 1, 1, 2)
 
         w_rows = [keep.tile([P, N], F32, name="w_rows%d" % b) for b in range(2)]
         w_banks = {}
         for nb in range(2):
             for kb in range(2):
-                w_banks[kb, nb] = psum.tile([P, P], F32, name="w_bank%d%d" % (kb, nb), tag="bank%d" % (2 * kb + nb))
+                w_banks[kb, nb] = psum.tile([P, P], F32, name="w_bank%d%d" % (kb, nb), tag="bank%d" % (2 * nb + kb))
             for a in range(PASSES):
                 cols = slice(a * P, (a + 1) * P)
                 for kb in range(2):

from contextlib import ExitStack

import concourse.mybir as mybir
from concourse.masks import make_identity

K, J, N, T, E = 256, 1024, 256, 2048, 128
SET = 8
FLOPS = 2 * K * J * N

F32 = mybir.dt.float32
BF16 = mybir.dt.bfloat16
U32 = mybir.dt.uint32
U16 = mybir.dt.uint16
U8 = mybir.dt.uint8
E4M3X4 = mybir.dt.float8_e4m3fn_x4
E5M2X4 = mybir.dt.float8_e5m2_x4
ALU = mybir.AluOpType
COPY = mybir.ActivationFunctionType.Copy

P = 128
PACK = 4
PASS = P * PACK
PASSES = J // PASS
LANES = 16
SETS = PASS // SET


def tile_list_moment_gaps_centred_columns_kernel(tc, xf, ra, gt, rb, old, offs, offs2, offs3, offs4, out):
    nc = tc.nc
    with ExitStack() as ctx:
        keep = ctx.enter_context(tc.tile_pool(name="keep", bufs=1))
        psum = ctx.enter_context(tc.psum_pool(name="psum", bufs=1))
        late = ctx.enter_context(tc.tile_pool(name="late", bufs=1))

        list1 = keep.tile([P, J // LANES], U16, name="list1")
        list2 = keep.tile([P, J // LANES], U16, name="list2")
        list3 = keep.tile([P, J // LANES], U16, name="list3")
        list4 = keep.tile([P, E // LANES], U16, name="list4")
        x_rows = [keep.tile([P, T], F32, name="x_rows%d" % b) for b in range(2)]
        g_rows = [keep.tile([P, T], F32, name="g_rows0"), late.tile([P, T], F32, name="g_rows1", offset=0, align_bytes=64)]
        ra_slots = keep.tile([P, PASSES, PACK], F32, name="ra_slots")
        rb_slots = keep.tile([P, PASSES, PACK], F32, name="rb_slots")
        old_rows = keep.tile([P, 2, E], F32, name="old_rows")

        nc.sync.dma_start(list2[:], offs2)
        nc.sync.dma_start(x_rows[0][:], xf[0:P, :])
        nc.sync.dma_start(list1[:], offs)
        nc.sync.dma_start(x_rows[1][:], xf[P : 2 * P, :])
        nc.sync.dma_start(ra_slots[:], ra.rearrange("o (a p t) -> p (o a) t", p=P, t=PACK))
        nc.sync.dma_start(list3[:], offs3)
        nc.sync.dma_start(g_rows[0][:], gt[0:P, :])
        nc.sync.dma_start(g_rows[1][:], gt[P : 2 * P, :])
        nc.sync.dma_start(rb_slots[:], rb.rearrange("o (a p t) -> p (o a) t", p=P, t=PACK))
        nc.sync.dma_start(list4[:], offs4)
        nc.sync.dma_start(old_rows[:], old.rearrange("(b p) e -> p b e", p=P))

        ident = keep.tile([P, P], F32, name="ident")
        make_identity(nc, ident[:])

        table_warm = keep.tile([P, 2], F32, name="table_warm")
        nc.vector.memset(table_warm[:, 0:1], 0.0)
        nc.scalar.activation(table_warm[:, 1:2], table_warm[:, 0:1], COPY)

        def picked(table, offsets, lo, hi):
            return table[:].indirect(offsets[:, lo // LANES : hi // LANES])

        ra_spread = []
        for a in range(PASSES):
            bank = psum.tile([P, PACK, P], F32, name="ra_spread%d" % a, tag="bank%d" % a)
            for t in range(PACK):
                nc.tensor.transpose(bank[:, t, :], ra_slots[:, a, t : t + 1].to_broadcast([P, P]), ident[:])
            ra_spread.append(bank)

        codes, scales, grouped = {}, {}, {}
        for side in "ug":
            for b in range(2):
                codes[side, b] = keep.tile([P, PASSES * P], U32, name="codes_%s%d" % (side, b), align_bytes=64)
                scales[side, b] = keep.tile([P, PASSES * P], U8, name="scales_%s%d" % (side, b), align_bytes=64)

        def quantise(side, b, first, last):
            cols = slice(first * P, last * P)
            nc.vector.quantize_mx(
                out=codes[side, b][:, cols].bitcast(E4M3X4 if side == "u" else E5M2X4),
                scales=scales[side, b][:, cols],
                in_=grouped[side, b, first],
            )

        gaps, pairs = {}, {}
        for b in range(2):
            second = keep.tile([P, J], F32, name="second%d" % b)
            gap = keep.tile([P, J], F32, name="gap%d" % b)
            cuts = [0, 128, PASS, J] if b == 0 else [0, PASS, J]
            for lo, hi in zip(cuts, cuts[1:]):
                nc.scalar.activation(second[:, lo:hi], picked(x_rows[b], list2, lo, hi), COPY)
                nc.vector.tensor_tensor(gap[:, lo:hi], picked(x_rows[b], list1, lo, hi), second[:, lo:hi], ALU.subtract)
            gaps[b] = gap

        def weigh_u(b, a):
            rounded = keep.tile([P, PASS], BF16, name="rounded_u%d%d" % (b, a), align_bytes=64)
            nc.vector.tensor_tensor(
                rounded[:].rearrange("r (u p e) -> r u p e", u=2, e=2),
                gaps[b][:, a * PASS : (a + 1) * PASS].rearrange("r (p u e) -> r u p e", u=2, e=2),
                ra_spread[a][:].rearrange("r (u e) p -> r u p e", u=2),
                ALU.mult,
            )
            pairs[b, a] = rounded[:].bitcast(F32)

        def turn_u(b):
            bank = psum.tile([P, PASSES, 2, P], F32, name="turned_u%d" % b, tag="bank%d" % (2 + b))
            for a in range(PASSES):
                for u in range(2):
                    nc.tensor.transpose(bank[:, a, u, :], pairs[b, a][:, u * P : (u + 1) * P], ident[:])
            words = late.tile([P, PASS], F32, name="grouped_u%d" % b, align_bytes=64, offset=b * PASS * 4)
            nc.scalar.copy(
                words[:].rearrange("p (a c u) -> p a c u", a=PASSES, u=2), bank[:].rearrange("p a u c -> p a c u")
            )
            grouped["u", b, 0] = words[:].bitcast(BF16)

        gg, sums, g_banks = {}, {}, {}
        LAST = 4 * T

        def pick_g(b, a):
            if (b, a) == (1, 1):
                gg[b, a] = late.tile([P, PASS], F32, name="gg%d%d" % (b, a), align_bytes=64, offset=LAST)
            else:
                gg[b, a] = keep.tile([P, PASS], F32, name="gg%d%d" % (b, a))
            nc.scalar.activation(gg[b, a][:], picked(g_rows[b], list3, a * PASS, (a + 1) * PASS), COPY)
            sums[b, a] = keep.tile([P, SETS], F32, name="sums%d%d" % (b, a))
            nc.vector.tensor_reduce(
                sums[b, a][:], gg[b, a][:].rearrange("r (c s) -> r c s", s=SET), mybir.AxisListType.X, ALU.add
            )
            dealt = keep.tile([P, PASS], F32, name="dealt%d%d" % (b, a))
            nc.gpsimd.tensor_scalar(
                dealt[:].rearrange("r (t q i) -> r q t i", t=PACK, i=4),
                gg[b, a][:].rearrange("r (q i t) -> r q t i", t=PACK, i=4),
                1.0,
                0.0,
                ALU.mult,
                ALU.add,
            )
            bank = psum.tile([P, PACK, P], F32, name="g_bank%d%d" % (b, a), tag="bank%d" % (4 + 2 * b + a))
            for t in range(PACK):
                nc.tensor.matmul(
                    bank[:, t, :], dealt[:, t * P : (t + 1) * P], ident[:], start=(t == 0), stop=False, is_transpose=True
                )
            g_banks[b, a] = bank

        def centre_g(b, a):
            place = 2 * PASS * 4 + (2 * b + a) * P * 4
            less_mean = late.tile([P, SETS, 2], F32, name="less_mean%d%d" % (b, a), align_bytes=64, offset=place)
            nc.scalar.activation(
                less_mean[:], sums[b, a][:].unsqueeze(2).to_broadcast([P, SETS, 2]), COPY, scale=-1.0 / SET
            )
            for t in range(PACK):
                nc.tensor.matmul(
                    g_banks[b, a][:, t, :],
                    less_mean[:].rearrange("r c h -> r (c h)"),
                    ident[:],
                    start=False,
                    stop=(t == PACK - 1),
                    is_transpose=True,
                )

        def weigh_g(b, a):
            name = "grouped_g%d%d" % (b, a)
            if b == 0:
                rounded = late.tile([P, PASS], BF16, name=name, align_bytes=64, offset=LAST + a * PASS * 2)
            else:
                rounded = keep.tile([P, PASS], BF16, name=name, align_bytes=64)
            nc.vector.tensor_tensor(
                rounded[:].rearrange("p (c t) -> p c t", t=PACK),
                g_banks[b, a][:].rearrange("p t c -> p c t"),
                rb_slots[:, a : a + 1, :].to_broadcast([P, P, PACK]),
                ALU.mult,
            )
            grouped["g", b, a] = rounded[:]

        weigh_u(0, 0)
        weigh_u(0, 1)
        weigh_u(1, 0)
        weigh_u(1, 1)
        pick_g(0, 0)
        pick_g(0, 1)
        pick_g(1, 0)
        pick_g(1, 1)
        centre_g(0, 0)
        centre_g(0, 1)
        turn_u(0)
        centre_g(1, 0)
        centre_g(1, 1)
        turn_u(1)
        weigh_g(0, 0)
        weigh_g(0, 1)
        quantise("u", 0, 0, 2)
        weigh_g(1, 0)
        quantise("u", 1, 0, 2)
        quantise("g", 0, 0, 1)
        quantise("g", 0, 1, 2)
        weigh_g(1, 1)
        quantise("g", 1, 0, 1)
        quantise("g", 1, 1, 2)

        w_rows = [keep.tile([P, N], F32, name="w_rows%d" % b) for b in range(2)]
        w_banks = {}
        for nb in range(2):
            for kb in range(2):
                w_banks[kb, nb] = psum.tile([P, P], F32, name="w_bank%d%d" % (kb, nb), tag="bank%d" % (2 * nb + kb))
            for a in range(PASSES):
                cols = slice(a * P, (a + 1) * P)
                for kb in range(2):
                    nc.tensor.matmul_mx(
                        out=w_banks[kb, nb][:],
                        lhsT=codes["u", kb][:, cols].bitcast(E4M3X4),
                        lhsT_scale=scales["u", kb][:, cols],
                        rhs=codes["g", nb][:, cols].bitcast(E5M2X4),
                        rhs_scale=scales["g", nb][:, cols],
                        start=(a == 0),
                        stop=(a == PASSES - 1),
                    )
        nc.scalar.copy(w_rows[0][:, 0:P], w_banks[0, 0][:])
        nc.scalar.copy(w_rows[1][:, 0:P], w_banks[1, 0][:])
        nc.scalar.copy(w_rows[0][:, P:N], w_banks[0, 1][:])
        nc.vector.tensor_copy(w_rows[1][:, P:N], w_banks[1, 1][:])

        w_picked = keep.tile([P, 2, E], F32, name="w_picked")
        nc.scalar.activation(w_picked[:, 0, :], w_rows[0][:].indirect(list4[:]), COPY)
        nc.vector.tensor_copy(w_picked[:, 1, :], w_rows[1][:].indirect(list4[:]))
        result = keep.tile([P, 2, E], F32, name="result")
        nc.vector.scalar_tensor_tensor(result[:], w_picked[:], 0.04, old_rows[:], ALU.mult, ALU.add)
        nc.sync.dma_start(out.rearrange("(b p) e -> p b e", p=P), result[:])
